import numpy as np
import ml_dtypes


def mxq(x, axis, fmt="e4m3"):
    dtype, down = {"e4m3": (ml_dtypes.float8_e4m3fn, 7), "e5m2": (ml_dtypes.float8_e5m2, 14)}[fmt]
    v = np.moveaxis(np.asarray(x, np.float32).astype(ml_dtypes.bfloat16).astype(np.float64), axis, -1)
    blocks = v.reshape(v.shape[:-1] + (-1, 32))
    amax = np.abs(blocks).max(-1, keepdims=True)
    byte = np.maximum(np.where(amax > 0, np.frexp(amax)[1] - 1 + 127, 0) - down, 1)
    scale = np.exp2(byte - 127.0)
    codes = (blocks / scale).astype(np.float32).astype(dtype).astype(np.float64)
    return np.moveaxis((codes * scale).reshape(v.shape), -1, axis)


WIDE = False


def mx_kscale(k):
    if not WIDE:
        return np.ones(k)
    levels = np.array([10, -10, 5, -5, 0])
    if k % 512:
        return np.exp2(np.random.permutation(np.resize(levels, k // 32))).repeat(32)
    a = np.empty((k // 512, 16))
    for p in range(k // 512):
        a[p, :8] = np.random.permutation(np.resize(levels, 8))
        for g in range(8):
            far = levels[np.abs(levels - a[p, g]) >= 10]
            a[p, g + 8] = far[np.random.randint(len(far))]
    return np.exp2(a.ravel()).repeat(32)


def f64(x):
    return np.asarray(x).astype(np.float64)


def striped8(idx):
    return np.asarray(idx).reshape(8, -1, 16).transpose(0, 2, 1).reshape(128, -1).astype(np.uint16)


def unstriped8(offs):
    return offs.reshape(8, 16, -1).transpose(0, 2, 1).reshape(8, -1).astype(np.int64)


def pick8(x, idx, run):
    r = np.arange(len(x))
    return x[r[:, None], idx[r % (8 * run) // run]]


E2M1 = np.array([0.0, 0.5, 1.0, 1.5, 2.0, 3.0, 4.0, 6.0, -0.0, -0.5, -1.0, -1.5, -2.0, -3.0, -4.0, -6.0])


def pack_weight(w, fmt):
    k, n = w.shape
    w = f64(np.asarray(w, np.float32).astype(ml_dtypes.bfloat16)).reshape(k // 32, 32, n)
    amax = np.abs(w).max(1)
    if fmt == "e4m3":
        byte = np.frexp(amax)[1] - 1 + 127 - 7
    else:
        mant, ex = np.frexp(amax / 6.0)
        byte = np.where(mant > 0.5, ex, ex - 1) + 127
    byte = np.clip(np.where(amax > 0, byte, 1), 1, 254)
    scaled = (w * np.exp2(127.0 - byte)[:, None, :]).reshape(k, n).astype(np.float32)
    by_word = np.ascontiguousarray(scaled.reshape(k // 512, 128, 4, n).transpose(0, 1, 3, 2))
    if fmt == "e4m3":
        words = by_word.astype(ml_dtypes.float8_e4m3fn).view(np.uint8)
    else:
        c = by_word.astype(ml_dtypes.float4_e2m1fn).view(np.uint8) & 0xF
        words = (c[..., 0::2] | (c[..., 1::2] << 4)).reshape(k // 512, 128, 2 * n)
    return np.ascontiguousarray(words), np.ascontiguousarray(byte.astype(np.uint8).reshape(k // 512, 16, n))


def unpack_weight(words, scales, fmt):
    g, _, n = scales.shape
    words = np.ascontiguousarray(words).reshape(g, 128, n, -1)
    if fmt == "e4m3":
        vals = words.view(ml_dtypes.float8_e4m3fn).astype(np.float64)
    else:
        nib = np.empty((g, 128, n, 4), np.uint8)
        nib[..., 0::2] = words & 0xF
        nib[..., 1::2] = words >> 4
        vals = E2M1[nib]
    vals = vals * np.repeat(np.exp2(scales.astype(np.float64) - 127.0), 8, axis=1)[..., None]
    return vals.transpose(0, 1, 3, 2).reshape(g * 512, n)


D, K, T, I, Q = 512, 512, 1024, 512, 128


def setup_inputs():
    n = np.random.standard_normal
    idx = np.stack([np.random.permutation(T)[:I] for _ in range(8)])
    idx2 = np.stack([np.random.permutation(T)[:I] for _ in range(8)])
    idx3 = np.stack([np.random.permutation(T)[:I] for _ in range(8)])
    idx4 = np.stack([np.random.permutation(T)[:I] for _ in range(8)])
    fd = mx_kscale(D)
    fk = mx_kscale(K)
    wqp = pack_weight(n((D, K)) * 1.0 / np.sqrt(D) * fd[:, None] * fk, "e4m3")
    keysp = pack_weight(n((K, T)) * 1.0 / np.sqrt(K) / fk[:, None], "e2m1")
    tagsp = pack_weight(n((D, T)) * 0.5 / np.sqrt(D) * fd[:, None], "e4m3")
    return {
        "states": (n((D, Q)) * 0.95 / fd[:, None]).astype(np.float32),
        "wq_words": wqp[0],
        "wq_scales": wqp[1],
        "keys_words": keysp[0],
        "keys_scales": keysp[1],
        "tags_words": tagsp[0],
        "tags_scales": tagsp[1],
        "offs": striped8(idx),
        "offs2": striped8(idx2),
        "offs3": striped8(idx3),
        "offs4": striped8(idx4),
    }


def reference(states, wq_words, wq_scales, keys_words, keys_scales, tags_words, tags_scales, offs, offs2, offs3, offs4):
    idx = unstriped8(offs)
    idx2 = unstriped8(offs2)
    idx3 = unstriped8(offs3)
    idx4 = unstriped8(offs4)
    wqu = unpack_weight(wq_words, wq_scales, "e4m3")
    keysu = unpack_weight(keys_words, keys_scales, "e2m1")
    tagsu = unpack_weight(tags_words, tags_scales, "e4m3")
    statesq = mxq(f64(states), 0, "e4m3")
    qv = wqu.T @ statesq
    qvq = mxq(qv, 0, "e4m3")
    a = qvq.T @ keysu + statesq.T @ tagsu
    lo1 = np.minimum(pick8(a, idx, 16), pick8(a, idx2, 16))
    r = pick8(a, idx, 16) - lo1
    f1 = np.zeros((Q, T))
    f1[np.arange(Q)[:, None], idx[np.arange(Q) % 128 // 16]] = r
    f2 = np.zeros((Q, T))
    f2[np.arange(Q)[:, None], idx2[np.arange(Q) % 128 // 16]] = r
    c1 = a - f1
    c2 = c1 + f2
    y = np.minimum(pick8(c2, idx3, 16), pick8(c2, idx4, 16))
    return y

@@ -1,0 +1,144 @@
+from contextlib import ExitStack
+
+import concourse.mybir as mybir
+
+F32 = mybir.dt.float32
+BF16 = mybir.dt.bfloat16
+I32 = mybir.dt.int32
+U32 = mybir.dt.uint32
+U16 = mybir.dt.uint16
+U8 = mybir.dt.uint8
+FP8X4 = mybir.dt.float8_e4m3fn_x4
+FP4X4 = mybir.dt.float4_e2m1fn_x4
+ALU = mybir.AluOpType
+ACT = mybir.ActivationFunctionType
+
+P = 128
+D, K, T, I, Q = 512, 512, 1024, 512, 128
+PACK = 4
+NB = 256
+H = I // 2
+HC = H // 16
+
+FLOPS = 2 * D * K * Q + 2 * K * Q * T + 2 * D * Q * T
+
+
+def tile_attend_bubbled_madeparts_kernel(tc, states, wq_words, wq_scales, keys_words, keys_scales,
+                                          tags_words, tags_scales, offs, offs2, offs3, offs4, out):
+    nc = tc.nc
+    with ExitStack() as ctx:
+        sb = ctx.enter_context(tc.tile_pool(name="sb", bufs=1))
+        ps = ctx.enter_context(tc.psum_pool(name="ps", bufs=1))
+
+        kt_rows = sb.tile([P, 4, T], U8, name="kt_rows", align_bytes=64)
+        wq_plane = sb.tile([P, K], U8, name="wq_plane", align_bytes=64)
+        f1 = sb.tile([P, T], F32, name="f1")
+        f2 = sb.tile([P, T], F32, name="f2")
+        nc.vector.memset(kt_rows[:].bitcast(I32), 0)
+        nc.vector.memset(wq_plane[:].bitcast(I32), 0)
+        nc.vector.memset(f1[:], 0.0)
+        nc.vector.memset(f2[:], 0.0)
+
+        wq_rows = sb.tile([4, 4, K], U8, name="wq_rows")
+        st_raw = sb.tile([P, PACK, Q], F32, name="st_raw")
+        wq_raw = sb.tile([P, K], I32, name="wq_raw")
+        keys_w = sb.tile([P, 2 * T], U8, name="keys_w", align_bytes=64)
+        tags_w = sb.tile([P, T], I32, name="tags_w", align_bytes=64)
+        lists = [sb.tile([P, I // 16], U16, name="list%d" % j) for j in range(4)]
+
+        def quadrant_major(scales):
+            return scales[0].bitcast(I32).rearrange("(g r) n -> r g n", r=4)
+
+        nc.sync.dma_start(out=wq_rows[:].bitcast(I32), in_=quadrant_major(wq_scales))
+        nc.sync.dma_start(out=st_raw[:], in_=states.rearrange("(p j) q -> p j q", j=PACK))
+        nc.sync.dma_start(out=wq_raw[:], in_=wq_words[0].rearrange("p n t -> p (n t)").bitcast(I32))
+        nc.sync.dma_start(out=kt_rows[4:8].bitcast(I32), in_=quadrant_major(tags_scales))
+        nc.sync.dma_start(out=kt_rows[0:4].bitcast(I32), in_=quadrant_major(keys_scales))
+        nc.sync.dma_start(out=tags_w[:], in_=tags_words[0].rearrange("p n t -> p (n t)").bitcast(I32))
+        nc.sync.dma_start(out=keys_w[:].bitcast(I32), in_=keys_words[0].bitcast(I32))
+        for tile, src in zip(lists, (offs, offs2, offs3, offs4)):
+            nc.sync.dma_start(tile[:], src)
+
+        for g in range(4):
+            nc.vector.tensor_copy(out=wq_plane[32 * g:32 * g + 4, :].bitcast(I32), in_=wq_rows[:, g, :].bitcast(I32))
+        wq_sc = sb.tile([P, PACK, P], U8, name="wq_sc", align_bytes=64)
+        nc.vector.tensor_copy(out=wq_sc[:], in_=wq_plane[:].rearrange("p (m t) -> p t m", t=PACK))
+
+        st_bf = sb.tile([P, Q, PACK], BF16, name="st_bf", align_bytes=64)
+        nc.vector.tensor_copy(out=st_bf[:].rearrange("p (c i) t -> p c t i", i=4),
+                              in_=st_raw[:].rearrange("p t (c i) -> p c t i", i=4))
+        st_q = sb.tile([P, Q], U32, name="st_q", align_bytes=64)
+        st_s = sb.tile([P, Q], U8, name="st_s", align_bytes=64)
+        nc.vector.quantize_mx(out=st_q[:].bitcast(FP8X4), scales=st_s[:],
+                              in_=st_bf[:].rearrange("p q t -> p (q t)"))
+
+        wq_w = sb.tile([P, PACK, P], I32, name="wq_w", align_bytes=64)
+        nc.vector.tensor_copy(out=wq_w[:].rearrange("p t (c i) -> p c t i", i=4),
+                              in_=wq_raw[:].rearrange("p (c i t) -> p c t i", i=4, t=PACK))
+
+        qv_ps = ps.tile([P, PACK, Q], F32, name="qv_ps")
+        for t in range(PACK):
+            nc.tensor.matmul_mx(out=qv_ps[:, t, :], lhsT=wq_w[:, t, :].bitcast(FP8X4), lhsT_scale=wq_sc[:, t, :],
+                                rhs=st_q[:].bitcast(FP8X4), rhs_scale=st_s[:], start=True, stop=True)
+
+        for g in range(1, 4):
+            nc.vector.tensor_copy(out=kt_rows[32 * g:32 * g + 32, 0, :].bitcast(I32),
+                                  in_=kt_rows[0:32, g, :].bitcast(I32))
+
+        banks = [ps.tile([P, NB], F32, name="a_ps%d" % b) for b in range(T // NB)]
+        for b, bank in enumerate(banks):
+            cols = slice(b * NB, (b + 1) * NB)
+            nc.tensor.matmul_mx(out=bank[:], lhsT=st_q[:].bitcast(FP8X4), lhsT_scale=st_s[:],
+                                rhs=tags_w[:, cols].bitcast(FP8X4), rhs_scale=kt_rows[4:P, 0, cols],
+                                start=True, stop=False)
+
+        qv_bf = sb.tile([P, Q, PACK], BF16, name="qv_bf", align_bytes=64)
+        nc.vector.tensor_copy(out=qv_bf[:], in_=qv_ps[:].rearrange("p t q -> p q t"))
+        qv_q = sb.tile([P, Q], U32, name="qv_q", align_bytes=64)
+        qv_s = sb.tile([P, Q], U8, name="qv_s", align_bytes=64)
+        nc.vector.quantize_mx(out=qv_q[:].bitcast(FP8X4), scales=qv_s[:],
+                              in_=qv_bf[:].rearrange("p q t -> p (q t)"))
+
+        a = sb.tile([P, T], F32, name="a")
+        for b, bank in enumerate(banks):
+            cols = slice(b * NB, (b + 1) * NB)
+            nc.tensor.matmul_mx(out=bank[:], lhsT=qv_q[:].bitcast(FP8X4), lhsT_scale=qv_s[:],
+                                rhs=keys_w[:, 2 * b * NB:2 * (b + 1) * NB].bitcast(FP4X4),
+                                rhs_scale=kt_rows[:, 0, cols], start=False, stop=True)
+            if b % 2 == 0:
+                nc.scalar.activation(out=a[:, cols], in_=bank[:], func=ACT.Copy)
+            else:
+                nc.vector.tensor_copy(out=a[:, cols], in_=bank[:])
+
+        def half(j, h):
+            return lists[j][:, h * HC:(h + 1) * HC]
+
+        g1 = [sb.tile([P, H], F32, name="g1_%d" % h) for h in range(2)]
+        g2 = [sb.tile([P, H], F32, name="g2_%d" % h) for h in range(2)]
+        dd = [sb.tile([P, H], F32, name="dd_%d" % h) for h in range(2)]
+        r = sb.tile([P, I], F32, name="r")
+        nc.vector.tensor_copy(out=g1[0][:], in_=a[:].indirect(half(0, 0)))
+        nc.scalar.activation(out=g2[0][:], in_=a[:].indirect(half(1, 0)), func=ACT.Copy)
+        nc.scalar.activation(out=g1[1][:], in_=a[:].indirect(half(0, 1)), func=ACT.Copy)
+        nc.scalar.activation(out=g2[1][:], in_=a[:].indirect(half(1, 1)), func=ACT.Copy)
+        nc.vector.tensor_tensor(out=dd[0][:], in0=g1[0][:], in1=g2[0][:], op=ALU.subtract)
+        nc.vector.tensor_scalar(out=r[:, 0:H], in0=dd[0][:], scalar1=0.0, scalar2=None, op0=ALU.max)
+        nc.vector.tensor_copy(out=f1[:].indirect(half(0, 0)), in_=r[:, 0:H])
+        nc.gpsimd.tensor_tensor(out=dd[1][:], in0=g1[1][:], in1=g2[1][:], op=ALU.subtract)
+        nc.gpsimd.tensor_scalar(out=r[:, H:I], in0=dd[1][:], scalar1=0.0, scalar2=0.0, op0=ALU.max, op1=ALU.add)
+        nc.vector.tensor_copy(out=f1[:].indirect(half(0, 1)), in_=r[:, H:I])
+        nc.vector.tensor_copy(out=f2[:].indirect(lists[1][:]), in_=r[:])
+        c1 = sb.tile([P, T], F32, name="c1")
+        nc.gpsimd.tensor_tensor(out=c1[:], in0=a[:], in1=f1[:], op=ALU.subtract)
+        c2 = sb.tile([P, T], F32, name="c2")
+        nc.vector.tensor_tensor(out=c2[:], in0=c1[:], in1=f2[:], op=ALU.add)
+
+        g3 = [sb.tile([P, H], F32, name="g3_%d" % h) for h in range(2)]
+        g4 = [sb.tile([P, H], F32, name="g4_%d" % h) for h in range(2)]
+        y = [sb.tile([P, H], F32, name="y_%d" % h) for h in range(2)]
+        for h in range(2):
+            nc.vector.tensor_copy(out=g3[h][:], in_=c2[:].indirect(half(2, h)))
+            nc.scalar.activation(out=g4[h][:], in_=c2[:].indirect(half(3, h)), func=ACT.Copy)
+        for h in range(2):
+            nc.vector.tensor_tensor(out=y[h][:], in0=g3[h][:], in1=g4[h][:], op=ALU.min)
+            nc.sync.dma_start(out=out[:, h * H:(h + 1) * H], in_=y[h][:])

@@ -1,6 +1,7 @@
 from contextlib import ExitStack
 
 import concourse.mybir as mybir
+from concourse.masks import make_identity
 
 F32 = mybir.dt.float32
 BF16 = mybir.dt.bfloat16
@@ -30,16 +31,20 @@ def tile_attend_bubbled_madeparts_kernel(tc, states, wq_words, wq_scales, keys_w
         sb = ctx.enter_context(tc.tile_pool(name="sb", bufs=1))
         ps = ctx.enter_context(tc.psum_pool(name="ps", bufs=1))
 
-        kt_rows = sb.tile([P, 4, T], U8, name="kt_rows", align_bytes=64)
+        keys_plane = sb.tile([P, T], U8, name="keys_plane", align_bytes=64)
+        tags_plane = sb.tile([P, T], U8, name="tags_plane", align_bytes=64)
         wq_plane = sb.tile([P, K], U8, name="wq_plane", align_bytes=64)
         f1 = sb.tile([P, T], F32, name="f1")
         f2 = sb.tile([P, T], F32, name="f2")
-        nc.vector.memset(kt_rows[:].bitcast(I32), 0)
+        nc.vector.memset(tags_plane[:].bitcast(I32), 0)
+        nc.vector.memset(keys_plane[:].bitcast(I32), 0)
         nc.vector.memset(wq_plane[:].bitcast(I32), 0)
         nc.vector.memset(f1[:], 0.0)
         nc.vector.memset(f2[:], 0.0)
 
         wq_rows = sb.tile([4, 4, K], U8, name="wq_rows")
+        ident = sb.tile([P, P], F32, name="ident")
+        make_identity(nc, ident[:])
         st_raw = sb.tile([P, PACK, Q], F32, name="st_raw")
         wq_raw = sb.tile([P, K], I32, name="wq_raw")
         keys_w = sb.tile([P, 2 * T], U8, name="keys_w", align_bytes=64)
@@ -49,51 +54,56 @@ def tile_attend_bubbled_madeparts_kernel(tc, states, wq_words, wq_scales, keys_w
         def quadrant_major(scales):
             return scales[0].bitcast(I32).rearrange("(g r) n -> r g n", r=4)
 
+        def load_plane(plane, scales):
+            for g in range(4):
+                nc.sync.dma_start(out=plane[32 * g:32 * g + 4, :].bitcast(I32),
+                                  in_=scales[0, 4 * g:4 * g + 4, :].bitcast(I32))
+
         nc.sync.dma_start(out=wq_rows[:].bitcast(I32), in_=quadrant_major(wq_scales))
         nc.sync.dma_start(out=st_raw[:], in_=states.rearrange("(p j) q -> p j q", j=PACK))
         nc.sync.dma_start(out=wq_raw[:], in_=wq_words[0].rearrange("p n t -> p (n t)").bitcast(I32))
-        nc.sync.dma_start(out=kt_rows[4:8].bitcast(I32), in_=quadrant_major(tags_scales))
-        nc.sync.dma_start(out=kt_rows[0:4].bitcast(I32), in_=quadrant_major(keys_scales))
+        load_plane(tags_plane, tags_scales)
         nc.sync.dma_start(out=tags_w[:], in_=tags_words[0].rearrange("p n t -> p (n t)").bitcast(I32))
         nc.sync.dma_start(out=keys_w[:].bitcast(I32), in_=keys_words[0].bitcast(I32))
+        load_plane(keys_plane, keys_scales)
         for tile, src in zip(lists, (offs, offs2, offs3, offs4)):
             nc.sync.dma_start(tile[:], src)
 
-        for g in range(4):
-            nc.vector.tensor_copy(out=wq_plane[32 * g:32 * g + 4, :].bitcast(I32), in_=wq_rows[:, g, :].bitcast(I32))
+        def spread(plane, rows):
+            for g in range(4):
+                nc.vector.tensor_copy(out=plane[32 * g:32 * g + 4, :].bitcast(I32), in_=rows[:, g, :].bitcast(I32))
+
+        spread(wq_plane, wq_rows)
         wq_sc = sb.tile([P, PACK, P], U8, name="wq_sc", align_bytes=64)
         nc.vector.tensor_copy(out=wq_sc[:], in_=wq_plane[:].rearrange("p (m t) -> p t m", t=PACK))
 
         st_bf = sb.tile([P, Q, PACK], BF16, name="st_bf", align_bytes=64)
-        nc.vector.tensor_copy(out=st_bf[:].rearrange("p (c i) t -> p c t i", i=4),
-                              in_=st_raw[:].rearrange("p t (c i) -> p c t i", i=4))
+        nc.scalar.activation(out=st_bf[:].rearrange("p (c i) t -> p c t i", i=4),
+                             in_=st_raw[:].rearrange("p t (c i) -> p c t i", i=4), func=ACT.Copy)
+        wq_w = sb.tile([P, PACK, P], I32, name="wq_w", align_bytes=64)
+        nc.vector.tensor_copy(out=wq_w[:].rearrange("p t (c i) -> p c t i", i=4),
+                              in_=wq_raw[:].rearrange("p (c i t) -> p c t i", i=4, t=PACK))
         st_q = sb.tile([P, Q], U32, name="st_q", align_bytes=64)
         st_s = sb.tile([P, Q], U8, name="st_s", align_bytes=64)
         nc.vector.quantize_mx(out=st_q[:].bitcast(FP8X4), scales=st_s[:],
                               in_=st_bf[:].rearrange("p q t -> p (q t)"))
 
-        wq_w = sb.tile([P, PACK, P], I32, name="wq_w", align_bytes=64)
-        nc.vector.tensor_copy(out=wq_w[:].rearrange("p t (c i) -> p c t i", i=4),
-                              in_=wq_raw[:].rearrange("p (c i t) -> p c t i", i=4, t=PACK))
-
-        qv_ps = ps.tile([P, PACK, Q], F32, name="qv_ps")
+        qv_ps = [ps.tile([P, 2, Q], F32, name="qv_ps%d" % u, tag="back%d" % u) for u in range(2)]
         for t in range(PACK):
-            nc.tensor.matmul_mx(out=qv_ps[:, t, :], lhsT=wq_w[:, t, :].bitcast(FP8X4), lhsT_scale=wq_sc[:, t, :],
+            nc.tensor.matmul_mx(out=qv_ps[t // 2][:, t % 2, :], lhsT=wq_w[:, t, :].bitcast(FP8X4), lhsT_scale=wq_sc[:, t, :],
                                 rhs=st_q[:].bitcast(FP8X4), rhs_scale=st_s[:], start=True, stop=True)
 
-        for g in range(1, 4):
-            nc.vector.tensor_copy(out=kt_rows[32 * g:32 * g + 32, 0, :].bitcast(I32),
-                                  in_=kt_rows[0:32, g, :].bitcast(I32))
 
         banks = [ps.tile([P, NB], F32, name="a_ps%d" % b) for b in range(T // NB)]
         for b, bank in enumerate(banks):
             cols = slice(b * NB, (b + 1) * NB)
             nc.tensor.matmul_mx(out=bank[:], lhsT=st_q[:].bitcast(FP8X4), lhsT_scale=st_s[:],
-                                rhs=tags_w[:, cols].bitcast(FP8X4), rhs_scale=kt_rows[4:P, 0, cols],
+                                rhs=tags_w[:, cols].bitcast(FP8X4), rhs_scale=tags_plane[:, cols],
                                 start=True, stop=False)
 
         qv_bf = sb.tile([P, Q, PACK], BF16, name="qv_bf", align_bytes=64)
-        nc.vector.tensor_copy(out=qv_bf[:], in_=qv_ps[:].rearrange("p t q -> p q t"))
+        nc.scalar.activation(out=qv_bf[:, :, 0:2], in_=qv_ps[0][:].rearrange("p t q -> p q t"), func=ACT.Copy)
+        nc.vector.tensor_copy(out=qv_bf[:, :, 2:4], in_=qv_ps[1][:].rearrange("p t q -> p q t"))
         qv_q = sb.tile([P, Q], U32, name="qv_q", align_bytes=64)
         qv_s = sb.tile([P, Q], U8, name="qv_s", align_bytes=64)
         nc.vector.quantize_mx(out=qv_q[:].bitcast(FP8X4), scales=qv_s[:],
@@ -104,7 +114,7 @@ def tile_attend_bubbled_madeparts_kernel(tc, states, wq_words, wq_scales, keys_w
             cols = slice(b * NB, (b + 1) * NB)
             nc.tensor.matmul_mx(out=bank[:], lhsT=qv_q[:].bitcast(FP8X4), lhsT_scale=qv_s[:],
                                 rhs=keys_w[:, 2 * b * NB:2 * (b + 1) * NB].bitcast(FP4X4),
-                                rhs_scale=kt_rows[:, 0, cols], start=False, stop=True)
+                                rhs_scale=keys_plane[:, cols], start=False, stop=True)
             if b % 2 == 0:
                 nc.scalar.activation(out=a[:, cols], in_=bank[:], func=ACT.Copy)
             else:
@@ -113,32 +123,52 @@ def tile_attend_bubbled_madeparts_kernel(tc, states, wq_words, wq_scales, keys_w
         def half(j, h):
             return lists[j][:, h * HC:(h + 1) * HC]
 
-        g1 = [sb.tile([P, H], F32, name="g1_%d" % h) for h in range(2)]
-        g2 = [sb.tile([P, H], F32, name="g2_%d" % h) for h in range(2)]
-        dd = [sb.tile([P, H], F32, name="dd_%d" % h) for h in range(2)]
+        halves = (slice(0, H), slice(H, I))
+        g1 = sb.tile([P, I], F32, name="g1")
+        g2 = sb.tile([P, I], F32, name="g2")
+        dd = sb.tile([P, I], F32, name="dd")
         r = sb.tile([P, I], F32, name="r")
-        nc.vector.tensor_copy(out=g1[0][:], in_=a[:].indirect(half(0, 0)))
-        nc.scalar.activation(out=g2[0][:], in_=a[:].indirect(half(1, 0)), func=ACT.Copy)
-        nc.scalar.activation(out=g1[1][:], in_=a[:].indirect(half(0, 1)), func=ACT.Copy)
-        nc.scalar.activation(out=g2[1][:], in_=a[:].indirect(half(1, 1)), func=ACT.Copy)
-        nc.vector.tensor_tensor(out=dd[0][:], in0=g1[0][:], in1=g2[0][:], op=ALU.subtract)
-        nc.vector.tensor_scalar(out=r[:, 0:H], in0=dd[0][:], scalar1=0.0, scalar2=None, op0=ALU.max)
-        nc.vector.tensor_copy(out=f1[:].indirect(half(0, 0)), in_=r[:, 0:H])
-        nc.gpsimd.tensor_tensor(out=dd[1][:], in0=g1[1][:], in1=g2[1][:], op=ALU.subtract)
-        nc.gpsimd.tensor_scalar(out=r[:, H:I], in0=dd[1][:], scalar1=0.0, scalar2=0.0, op0=ALU.max, op1=ALU.add)
-        nc.vector.tensor_copy(out=f1[:].indirect(half(0, 1)), in_=r[:, H:I])
-        nc.vector.tensor_copy(out=f2[:].indirect(lists[1][:]), in_=r[:])
-        c1 = sb.tile([P, T], F32, name="c1")
-        nc.gpsimd.tensor_tensor(out=c1[:], in0=a[:], in1=f1[:], op=ALU.subtract)
-        c2 = sb.tile([P, T], F32, name="c2")
-        nc.vector.tensor_tensor(out=c2[:], in0=c1[:], in1=f2[:], op=ALU.add)
+        nc.vector.tensor_copy(out=g2[:], in_=a[:].indirect(lists[1][:]))
+        for h, part in enumerate(halves):
+            nc.scalar.activation(out=g1[:, part], in_=a[:].indirect(half(0, h)), func=ACT.Copy)
 
-        g3 = [sb.tile([P, H], F32, name="g3_%d" % h) for h in range(2)]
-        g4 = [sb.tile([P, H], F32, name="g4_%d" % h) for h in range(2)]
-        y = [sb.tile([P, H], F32, name="y_%d" % h) for h in range(2)]
-        for h in range(2):
-            nc.vector.tensor_copy(out=g3[h][:], in_=c2[:].indirect(half(2, h)))
-            nc.scalar.activation(out=g4[h][:], in_=c2[:].indirect(half(3, h)), func=ACT.Copy)
-        for h in range(2):
-            nc.vector.tensor_tensor(out=y[h][:], in0=g3[h][:], in1=g4[h][:], op=ALU.min)
-            nc.sync.dma_start(out=out[:, h * H:(h + 1) * H], in_=y[h][:])
+        turned = [ps.tile([P, 4, P], F32, name="turned%d" % u) for u in range(2)]
+        for u in range(2):
+            for j in range(4):
+                blk = slice((4 * u + j) * P, (4 * u + j + 1) * P)
+                nc.tensor.matmul(turned[u][:, j, :], lhsT=a[:, blk], rhs=ident[:], is_transpose=True,
+                                 start=(j == 0), stop=False)
+
+        for part in halves:
+            nc.vector.tensor_tensor(out=dd[:, part], in0=g1[:, part], in1=g2[:, part], op=ALU.subtract)
+        for part in halves:
+            nc.vector.tensor_scalar(out=r[:, part], in0=dd[:, part], scalar1=0.0, scalar2=None, op0=ALU.max)
+        nc.vector.tensor_copy(out=f2[:].indirect(lists[1][:]), in_=r[:])
+        nc.vector.tensor_copy(out=f1[:].indirect(lists[0][:]), in_=r[:])
+
+        c2 = sb.tile([P, T], F32, name="c2")
+        for u in range(2):
+            for j in range(4):
+                blk = slice((4 * u + j) * P, (4 * u + j + 1) * P)
+                nc.tensor.matmul(turned[u][:, j, :], lhsT=f2[:, blk], rhs=ident[:], is_transpose=True,
+                                 start=False, stop=(j == 3))
+        sum_t = [sb.tile([P, 4, P], F32, name="sum_t%d" % u) for u in range(2)]
+        for u in range(2):
+            nc.scalar.activation(out=sum_t[u][:], in_=turned[u][:], func=ACT.Copy)
+        for u in range(2):
+            back = ps.tile([P, 4, P], F32, name="back%d" % u, tag="back%d" % u)
+            for j in range(4):
+                nc.tensor.transpose(back[:, j, :], sum_t[u][:, j, :], ident[:])
+            cols = slice(u * 4 * P, (u + 1) * 4 * P)
+            nc.vector.tensor_tensor(out=c2[:, cols], in0=back[:].rearrange("p j n -> p (j n)"), in1=f1[:, cols],
+                                    op=ALU.subtract)
+
+        g3 = sb.tile([P, I], F32, name="g3")
+        g4 = sb.tile([P, I], F32, name="g4")
+        y = sb.tile([P, I], F32, name="y")
+        nc.vector.tensor_copy(out=g3[:], in_=c2[:].indirect(lists[2][:]))
+        for h, part in enumerate(halves):
+            nc.scalar.activation(out=g4[:, part], in_=c2[:].indirect(half(3, h)), func=ACT.Copy)
+        for part in halves:
+            nc.vector.tensor_tensor(out=y[:, part], in0=g3[:, part], in1=g4[:, part], op=ALU.min)
+            nc.sync.dma_start(out=out[:, part], in_=y[:, part])

from contextlib import ExitStack

import concourse.mybir as mybir
from concourse.masks import make_identity

F32 = mybir.dt.float32
BF16 = mybir.dt.bfloat16
I32 = mybir.dt.int32
U32 = mybir.dt.uint32
U16 = mybir.dt.uint16
U8 = mybir.dt.uint8
FP8X4 = mybir.dt.float8_e4m3fn_x4
FP4X4 = mybir.dt.float4_e2m1fn_x4
ALU = mybir.AluOpType
ACT = mybir.ActivationFunctionType

P = 128
D, K, T, I, Q = 512, 512, 1024, 512, 128
PACK = 4
NB = 256
H = I // 2
HC = H // 16

FLOPS = 2 * D * K * Q + 2 * K * Q * T + 2 * D * Q * T


def tile_attend_bubbled_madeparts_kernel(tc, states, wq_words, wq_scales, keys_words, keys_scales,
                                          tags_words, tags_scales, offs, offs2, offs3, offs4, out):
    nc = tc.nc
    with ExitStack() as ctx:
        sb = ctx.enter_context(tc.tile_pool(name="sb", bufs=1))
        ps = ctx.enter_context(tc.psum_pool(name="ps", bufs=1))

        keys_plane = sb.tile([P, T], U8, name="keys_plane", align_bytes=64)
        tags_plane = sb.tile([P, T], U8, name="tags_plane", align_bytes=64)
        wq_plane = sb.tile([P, K], U8, name="wq_plane", align_bytes=64)
        f1 = sb.tile([P, T], F32, name="f1")
        f2 = sb.tile([P, T], F32, name="f2")
        nc.vector.memset(tags_plane[:].bitcast(I32), 0)
        nc.vector.memset(keys_plane[:].bitcast(I32), 0)
        nc.vector.memset(wq_plane[:].bitcast(I32), 0)
        nc.vector.memset(f1[:], 0.0)
        nc.vector.memset(f2[:], 0.0)

        wq_rows = sb.tile([4, 4, K], U8, name="wq_rows")
        ident = sb.tile([P, P], F32, name="ident")
        make_identity(nc, ident[:])
        st_raw = sb.tile([P, PACK, Q], F32, name="st_raw")
        wq_raw = sb.tile([P, K], I32, name="wq_raw")
        keys_w = sb.tile([P, 2 * T], U8, name="keys_w", align_bytes=64)
        tags_w = sb.tile([P, T], I32, name="tags_w", align_bytes=64)
        lists = [sb.tile([P, I // 16], U16, name="list%d" % j) for j in range(4)]

        def quadrant_major(scales):
            return scales[0].bitcast(I32).rearrange("(g r) n -> r g n", r=4)

        def load_plane(plane, scales):
            for g in range(4):
                nc.sync.dma_start(out=plane[32 * g:32 * g + 4, :].bitcast(I32),
                                  in_=scales[0, 4 * g:4 * g + 4, :].bitcast(I32))

        nc.sync.dma_start(out=wq_rows[:].bitcast(I32), in_=quadrant_major(wq_scales))
        nc.sync.dma_start(out=st_raw[:], in_=states.rearrange("(p j) q -> p j q", j=PACK))
        nc.sync.dma_start(out=wq_raw[:], in_=wq_words[0].rearrange("p n t -> p (n t)").bitcast(I32))
        load_plane(tags_plane, tags_scales)
        nc.sync.dma_start(out=tags_w[:], in_=tags_words[0].rearrange("p n t -> p (n t)").bitcast(I32))
        nc.sync.dma_start(out=keys_w[:].bitcast(I32), in_=keys_words[0].bitcast(I32))
        load_plane(keys_plane, keys_scales)
        for tile, src in zip(lists, (offs, offs2, offs3, offs4)):
            nc.sync.dma_start(tile[:], src)

        def spread(plane, rows):
            for g in range(4):
                nc.vector.tensor_copy(out=plane[32 * g:32 * g + 4, :].bitcast(I32), in_=rows[:, g, :].bitcast(I32))

        spread(wq_plane, wq_rows)
        wq_sc = sb.tile([P, PACK, P], U8, name="wq_sc", align_bytes=64)
        nc.vector.tensor_copy(out=wq_sc[:], in_=wq_plane[:].rearrange("p (m t) -> p t m", t=PACK))

        st_bf = sb.tile([P, Q, PACK], BF16, name="st_bf", align_bytes=64)
        nc.scalar.activation(out=st_bf[:].rearrange("p (c i) t -> p c t i", i=4),
                             in_=st_raw[:].rearrange("p t (c i) -> p c t i", i=4), func=ACT.Copy)
        wq_w = sb.tile([P, PACK, P], I32, name="wq_w", align_bytes=64)
        nc.vector.tensor_copy(out=wq_w[:].rearrange("p t (c i) -> p c t i", i=4),
                              in_=wq_raw[:].rearrange("p (c i t) -> p c t i", i=4, t=PACK))
        st_q = sb.tile([P, Q], U32, name="st_q", align_bytes=64)
        st_s = sb.tile([P, Q], U8, name="st_s", align_bytes=64)
        nc.vector.quantize_mx(out=st_q[:].bitcast(FP8X4), scales=st_s[:],
                              in_=st_bf[:].rearrange("p q t -> p (q t)"))

        qv_ps = [ps.tile([P, 2, Q], F32, name="qv_ps%d" % u, tag="back%d" % u) for u in range(2)]
        for t in range(PACK):
            nc.tensor.matmul_mx(out=qv_ps[t // 2][:, t % 2, :], lhsT=wq_w[:, t, :].bitcast(FP8X4), lhsT_scale=wq_sc[:, t, :],
                                rhs=st_q[:].bitcast(FP8X4), rhs_scale=st_s[:], start=True, stop=True)


        banks = [ps.tile([P, NB], F32, name="a_ps%d" % b) for b in range(T // NB)]
        for b, bank in enumerate(banks):
            cols = slice(b * NB, (b + 1) * NB)
            nc.tensor.matmul_mx(out=bank[:], lhsT=st_q[:].bitcast(FP8X4), lhsT_scale=st_s[:],
                                rhs=tags_w[:, cols].bitcast(FP8X4), rhs_scale=tags_plane[:, cols],
                                start=True, stop=False)

        qv_bf = sb.tile([P, Q, PACK], BF16, name="qv_bf", align_bytes=64)
        nc.scalar.activation(out=qv_bf[:, :, 0:2], in_=qv_ps[0][:].rearrange("p t q -> p q t"), func=ACT.Copy)
        nc.vector.tensor_copy(out=qv_bf[:, :, 2:4], in_=qv_ps[1][:].rearrange("p t q -> p q t"))
        qv_q = sb.tile([P, Q], U32, name="qv_q", align_bytes=64)
        qv_s = sb.tile([P, Q], U8, name="qv_s", align_bytes=64)
        nc.vector.quantize_mx(out=qv_q[:].bitcast(FP8X4), scales=qv_s[:],
                              in_=qv_bf[:].rearrange("p q t -> p (q t)"))

        a = sb.tile([P, T], F32, name="a")
        for b, bank in enumerate(banks):
            cols = slice(b * NB, (b + 1) * NB)
            nc.tensor.matmul_mx(out=bank[:], lhsT=qv_q[:].bitcast(FP8X4), lhsT_scale=qv_s[:],
                                rhs=keys_w[:, 2 * b * NB:2 * (b + 1) * NB].bitcast(FP4X4),
                                rhs_scale=keys_plane[:, cols], start=False, stop=True)
            if b % 2 == 0:
                nc.scalar.activation(out=a[:, cols], in_=bank[:], func=ACT.Copy)
            else:
                nc.vector.tensor_copy(out=a[:, cols], in_=bank[:])

        def half(j, h):
            return lists[j][:, h * HC:(h + 1) * HC]

        halves = (slice(0, H), slice(H, I))
        g1 = sb.tile([P, I], F32, name="g1")
        g2 = sb.tile([P, I], F32, name="g2")
        dd = sb.tile([P, I], F32, name="dd")
        r = sb.tile([P, I], F32, name="r")
        nc.vector.tensor_copy(out=g2[:], in_=a[:].indirect(lists[1][:]))
        for h, part in enumerate(halves):
            nc.scalar.activation(out=g1[:, part], in_=a[:].indirect(half(0, h)), func=ACT.Copy)

        turned = [ps.tile([P, 4, P], F32, name="turned%d" % u) for u in range(2)]
        for u in range(2):
            for j in range(4):
                blk = slice((4 * u + j) * P, (4 * u + j + 1) * P)
                nc.tensor.matmul(turned[u][:, j, :], lhsT=a[:, blk], rhs=ident[:], is_transpose=True,
                                 start=(j == 0), stop=False)

        for part in halves:
            nc.vector.tensor_tensor(out=dd[:, part], in0=g1[:, part], in1=g2[:, part], op=ALU.subtract)
        for part in halves:
            nc.vector.tensor_scalar(out=r[:, part], in0=dd[:, part], scalar1=0.0, scalar2=None, op0=ALU.max)
        nc.vector.tensor_copy(out=f2[:].indirect(lists[1][:]), in_=r[:])
        nc.vector.tensor_copy(out=f1[:].indirect(lists[0][:]), in_=r[:])

        c2 = sb.tile([P, T], F32, name="c2")
        for u in range(2):
            for j in range(4):
                blk = slice((4 * u + j) * P, (4 * u + j + 1) * P)
                nc.tensor.matmul(turned[u][:, j, :], lhsT=f2[:, blk], rhs=ident[:], is_transpose=True,
                                 start=False, stop=(j == 3))
        sum_t = [sb.tile([P, 4, P], F32, name="sum_t%d" % u) for u in range(2)]
        for u in range(2):
            nc.scalar.activation(out=sum_t[u][:], in_=turned[u][:], func=ACT.Copy)
        for u in range(2):
            back = ps.tile([P, 4, P], F32, name="back%d" % u, tag="back%d" % u)
            for j in range(4):
                nc.tensor.transpose(back[:, j, :], sum_t[u][:, j, :], ident[:])
            cols = slice(u * 4 * P, (u + 1) * 4 * P)
            nc.vector.tensor_tensor(out=c2[:, cols], in0=back[:].rearrange("p j n -> p (j n)"), in1=f1[:, cols],
                                    op=ALU.subtract)

        g3 = sb.tile([P, I], F32, name="g3")
        g4 = sb.tile([P, I], F32, name="g4")
        y = sb.tile([P, I], F32, name="y")
        nc.vector.tensor_copy(out=g3[:], in_=c2[:].indirect(lists[2][:]))
        for h, part in enumerate(halves):
            nc.scalar.activation(out=g4[:, part], in_=c2[:].indirect(half(3, h)), func=ACT.Copy)
        for part in halves:
            nc.vector.tensor_tensor(out=y[:, part], in0=g3[:, part], in1=g4[:, part], op=ALU.min)
            nc.sync.dma_start(out=out[:, part], in_=y[:, part])
